import numpy as np, ml_dtypes
CORES = [56,61,80,85]
N = 4
import mx_ref
NC, G, GR = 256, 4, 2
C = np.float32(0.041)
BF = ml_dtypes.bfloat16
def cut(t, i, w=512):
    return t[:, w * i:w * i + w]
def tile(rs):
    return np.stack(rs, axis=2).reshape(128, -1).astype(BF)
def layer(w, X):
    out = []
    for i in range(G):
        for t in range(len(X)):
            p = mx_ref.matmul(mx_ref.quantize(cut(w, len(X) * i + t)), X[t])
            z = p if t == 0 else z + p
        out.append(z)
    return out
def act(Z):
    return [np.maximum(z, 0) * C for z in Z]
def setup_inputs(rng):
    def f(*shape):
        return mx_ref.flush((rng.standard_normal(shape, dtype=np.float32) * np.exp2(rng.integers(-2, 3, shape[:-1] + (1,)))).astype(BF))
    return {"xa": f(N, 128, 512), "xb": f(N, 128, 4 * NC), "wa": f(N, 128, G * 512), "wb": f(N, 128, G * 512)}
def setup_inputs_blocks(rng):
    d = setup_inputs(rng)
    for k in ("xa", "xb", "wa", "wb"): d[k] = mx_ref.spread(d[k], rng, 2)
    return d
def setup_inputs_wide(rng):
    d = setup_inputs(rng)
    for k in ("xa", "xb", "wa", "wb"): d[k] = mx_ref.flush((d[k].astype(np.float32) * np.exp2(rng.integers(-5, 6, (N, 1, 1))).astype(np.float32)).astype(BF))
    return d
def reference(xa, xb, wa, wb):
    A = [mx_ref.quantize(tile(act(layer(wa[j], [mx_ref.quantize(xa[j])])))) for j in range(N)]
    M = [mx_ref.quantize(tile(act(layer(wb[j], [mx_ref.quantize(xb[j])])))) for j in range(N)]
    y = np.zeros((N, 128, NC), np.float32)
    for r in range(N):
        i, j = divmod(r, GR)
        for k in range(GR):
            p = mx_ref.matmul(A[GR * i + k], M[GR * k + j])
            y[r] = p if k == 0 else y[r] + p
    return {"y": y}

@@ -1,0 +1,214 @@
+import numpy as np
+from concourse.bass import DstId, RemoteDMATransfer
+from concourse.mybir import dt, AluOpType, ActivationFunctionType
+
+GR = 2
+NA, NB, G = 128, 256, 4
+W = 4 * NA
+H = NB // 2
+CUT = NB - NB // 4
+C = float(np.float32(0.041))
+CORES_SIM = 96
+
+SCRATCH = {
+    "txa": ("sbuf", [128, 4 * NA], "bfloat16"),
+    "txb": ("sbuf", [128, 4 * NB], "bfloat16"),
+    "twa": ("sbuf", [128, G * W], "bfloat16"),
+    "twb": ("sbuf", [128, G * W], "bfloat16"),
+    "ta": ("sbuf", [128, 4 * NA], "bfloat16"),
+    "tb": ("sbuf", [128, 4 * NB], "bfloat16"),
+    "xaq": ("sbuf", [128, NA], "float8_e4m3fn_x4"), "xas": ("sbuf", [128, NA], "uint8"),
+    "xbq": ("sbuf", [128, NB], "float8_e4m3fn_x4"), "xbs": ("sbuf", [128, NB], "uint8"),
+    "waq": ("sbuf", [128, G * 128], "float8_e4m3fn_x4"), "was": ("sbuf", [128, G * 128], "uint8"),
+    "wbq": ("sbuf", [128, G * 128], "float8_e4m3fn_x4"), "wbs": ("sbuf", [128, G * 128], "uint8"),
+    "aq": ("sbuf", [128, NA], "float8_e4m3fn_x4"), "as_": ("sbuf", [128, NA], "uint8"),
+    "bq": ("sbuf", [128, NB], "float8_e4m3fn_x4"), "bs": ("sbuf", [128, NB], "uint8"),
+    "iaq": ("sbuf", [128, NA], "float8_e4m3fn_x4"), "ias": ("sbuf", [128, NA], "uint8"),
+    "ibq": ("sbuf", [128, NB], "float8_e4m3fn_x4"), "ibs": ("sbuf", [128, NB], "uint8"),
+    "rq": ("sbuf", [128, NB], "float8_e4m3fn_x4"), "rs": ("sbuf", [128, NB], "uint8"),
+    "yo": ("sbuf", [128, NB], "float32"),
+    "ps": ("psum", [128, 512 * 8], "float32"),
+}
+SEMAPHORES = (["lxb", "lwb01", "lwb2", "lwb3", "lxa", "lwa01", "lwa2", "lwa3"]
+              + ["qxb", "qxa", "qa", "qb"] + ["qwb%d" % i for i in range(G)] + ["qwa%d" % i for i in range(G)]
+              + ["mb0", "mb1", "mb2", "mb30", "mb31"] + ["ma%d" % i for i in range(G)] + ["rb", "ra"]
+              + ["y0", "y1", "c0", "c1", "st0", "st1", "left", "ain", "bin", "rin"])
+
+
+def engines(mask):
+    return [1 << e for e in range(mask.bit_length()) if mask >> e & 1]
+
+
+def relays_of(src, dst, cores, topo):
+    return [q for q in range(CORES_SIM) if q not in cores and topo.chip(q) == topo.chip(src)
+            and topo.die(q) == topo.die(src) and topo.may_write(q, dst)][:2]
+
+
+def did(core, topo):
+    rid, pid, _ = topo.addr(core)
+    return DstId(rid=rid, pnc=pid)
+
+
+def codes(buf, a, b):
+    return buf[:, a:b].bitcast(dt.uint8)
+
+
+def send_first(g, T, topo, src, dst, src_q, dst_q, sem, eng):
+    rid, pid, _ = topo.addr(dst)
+    g.remote_dma(codes(dst_q, 0, CUT), codes(src_q, 0, CUT), sem, T.sem.left, pid, rid, sum(eng))
+
+
+def send_rest(g, T, topo, src, dst, src_q, src_s, dst_q, dst_s, sem, eng):
+    h = len(eng) // 2
+    g.remote_dma_fused([
+        RemoteDMATransfer(dst_ids=[did(dst, topo)], dma_engine_mask=sum(eng[:h]), remote_sem=sem,
+                          src=codes(src_q, CUT, NB), dst=codes(dst_q, CUT, NB)),
+        RemoteDMATransfer(dst_ids=[did(dst, topo)], dma_engine_mask=sum(eng[h:]), remote_sem=sem,
+                          src=src_s[:, 0:NB], dst=dst_s[:, 0:NB]),
+    ], local_sem=T.sem.left)
+
+
+def rank_program(g, core, T, topo):
+    cores = list(T.cores)
+    rank = T.rank_of(core)
+    s = T.sem
+    if rank is None:
+        for r, src in enumerate(cores):
+            dst = cores[(r + GR) % (GR * GR)]
+            rel = relays_of(src, dst, cores, topo)
+            if core in rel:
+                eng = engines(topo.mask(core, dst))
+                n_in = len(engines(topo.mask(src, core))) // 2
+                g.wait_ge(s.rin, n_in)
+                if core == rel[0]:
+                    send_first(g, T, topo, core, dst, T.rq, T.ibq, s.bin, eng)
+                else:
+                    send_rest(g, T, topo, core, dst, T.rq, T.rs, T.ibq, T.ibs, s.bin, eng)
+                g.wait_ge(s.left, len(eng))
+        return
+
+    row, col = divmod(rank, GR)
+    row_mate = cores[GR * row + 1 - col]
+    col_mate = cores[GR * (1 - row) + col]
+    rel = relays_of(core, col_mate, cores, topo)
+    PS = T.ps
+
+    def bank(k, n):
+        return PS[:, 512 * k:512 * k + n]
+
+    g.sync.dma_start(T.txb[:], T.xb[:]).then_inc(s.lxb, 16)
+    g.scalar.dma_start(T.twb[:, 0:2 * W], T.wb[:, 0:2 * W]).then_inc(s.lwb01, 16)
+    g.sync.dma_start(T.twb[:, 2 * W:3 * W], T.wb[:, 2 * W:3 * W]).then_inc(s.lwb2, 16)
+    g.scalar.dma_start(T.twb[:, 3 * W:4 * W], T.wb[:, 3 * W:4 * W]).then_inc(s.lwb3, 16)
+    g.sync.dma_start(T.txa[:], T.xa[:]).then_inc(s.lxa, 16)
+    g.sync.dma_start(T.twa[:, 0:2 * W], T.wa[:, 0:2 * W]).then_inc(s.lwa01, 16)
+    g.sync.wait_ge(s.qb, 1)
+    g.sync.dma_start(T.twa[:, 2 * W:3 * W], T.wa[:, 2 * W:3 * W]).then_inc(s.lwa2, 16)
+    g.sync.dma_start(T.twa[:, 3 * W:4 * W], T.wa[:, 3 * W:4 * W]).then_inc(s.lwa3, 16)
+
+    v = g.vector
+
+    def vrelu(out, in_):
+        return v.tensor_scalar(out, in_, 0.0, C, AluOpType.max, AluOpType.mult)
+
+    def quant_w(which, i):
+        t, q, p = {"a": (T.twa, T.waq, T.was), "b": (T.twb, T.wbq, T.wbs)}[which]
+        v.quantize_mx(q[:, 128 * i:128 * i + 128], p[:, 128 * i:128 * i + 128],
+                      t[:, W * i:W * i + W]).then_inc(s["qw%s%d" % (which, i)], 1)
+
+    v.wait_ge(s.lxb, 16)
+    v.quantize_mx(T.xbq[:, 0:NB], T.xbs[:, 0:NB], T.txb[:, 0:4 * NB]).then_inc(s.qxb, 1)
+    v.wait_ge(s.lwb01, 16)
+    quant_w("b", 0)
+    quant_w("b", 1)
+    v.wait_ge(s.lwb2, 16)
+    quant_w("b", 2)
+    v.wait_ge(s.mb1, 1)
+    vrelu(T.tb[:, 1:4 * NB:4], bank(1, NB)).then_inc(s.rb, 1)
+    v.wait_ge(s.lwb3, 16)
+    quant_w("b", 3)
+    v.wait_ge(s.mb31, 1)
+    vrelu(T.tb[:, 4 * H + 3:4 * NB:4], bank(4, H)).then_inc(s.rb, 1)
+    v.wait_ge(s.rb, 5)
+    v.quantize_mx(T.bq[:, 0:NB], T.bs[:, 0:NB], T.tb[:, 0:4 * NB]).then_inc(s.qb, 1)
+    v.wait_ge(s.lxa, 16)
+    v.quantize_mx(T.xaq[:, 0:NA], T.xas[:, 0:NA], T.txa[:, 0:4 * NA]).then_inc(s.qxa, 1)
+    v.wait_ge(s.lwa01, 16)
+    quant_w("a", 0)
+    quant_w("a", 1)
+    v.wait_ge(s.lwa2, 16)
+    quant_w("a", 2)
+    v.wait_ge(s.lwa3, 16)
+    quant_w("a", 3)
+    v.wait_ge(s.ma3, 1)
+    vrelu(T.ta[:, 3:4 * NA:4], bank(0, NA)).then_inc(s.ra, 1)
+    v.wait_ge(s.ra, 4)
+    v.quantize_mx(T.aq[:, 0:NA], T.as_[:, 0:NA], T.ta[:, 0:4 * NA]).then_inc(s.qa, 1)
+    v.wait_ge(s.y0, 1)
+    v.tensor_copy(T.yo[:, 0:H], bank(1, H)).then_inc(s.c0, 1)
+
+    sc = g.scalar
+    relu, copy = ActivationFunctionType.Relu, ActivationFunctionType.Copy
+    sc.wait_ge(s.mb0, 1)
+    sc.activation(T.tb[:, 0:4 * NB:4], bank(0, NB), relu, scale=C).then_inc(s.rb, 1)
+    sc.wait_ge(s.mb2, 1)
+    sc.activation(T.tb[:, 2:4 * NB:4], bank(2, NB), relu, scale=C).then_inc(s.rb, 1)
+    sc.wait_ge(s.mb30, 1)
+    sc.activation(T.tb[:, 3:4 * H:4], bank(3, H), relu, scale=C).then_inc(s.rb, 1)
+    for i in range(G - 1):
+        sc.wait_ge(s["ma%d" % i], 1)
+        sc.activation(T.ta[:, i:4 * NA:4], bank(5 + i, NA), relu, scale=C).then_inc(s.ra, 1)
+    sc.wait_ge(s.y1, 1)
+    sc.activation(T.yo[:, H:NB], bank(2, H), copy).then_inc(s.c1, 1)
+    sc.wait_ge(s.c1, 1)
+    sc.dma_start(T.y[:, H:NB], T.yo[:, H:NB]).then_inc(s.st1, 16)
+    sc.wait_ge(s.st1, 16)
+
+    t = g.tensor
+
+    def mm(out, q, p, i, xq, xp, a, b, start=True, stop=True):
+        return t.matmul_mx(out, q[:, 128 * i:128 * i + 128], p[:, 128 * i:128 * i + 128],
+                           xq[:, a:b], xp[:, a:b], start, stop)
+
+    t.wait_ge(s.qxb, 1)
+    for i in range(G - 1):
+        t.wait_ge(s["qwb%d" % i], 1)
+        mm(bank(i, NB), T.wbq, T.wbs, i, T.xbq, T.xbs, 0, NB).then_inc(s["mb%d" % i], 1)
+    t.wait_ge(s.qwb3, 1)
+    mm(bank(3, H), T.wbq, T.wbs, 3, T.xbq, T.xbs, 0, H).then_inc(s.mb30, 1)
+    mm(bank(4, H), T.wbq, T.wbs, 3, T.xbq, T.xbs, H, NB).then_inc(s.mb31, 1)
+    t.wait_ge(s.qxa, 1)
+    t.wait_ge(s.rb, 5)
+    for i in range(G):
+        t.wait_ge(s["qwa%d" % i], 1)
+        mm(bank((5, 6, 7, 0)[i], NA), T.waq, T.was, i, T.xaq, T.xas, 0, NA).then_inc(s["ma%d" % i], 1)
+    a_of = {col: (T.aq, T.as_), 1 - col: (T.iaq, T.ias)}
+    t.wait_ge(s.qb, 1)
+    t.wait_ge(s.qa, 1)
+    n_a = 2 * len(engines(topo.mask(row_mate, core)))
+    if row != col:
+        t.wait_ge(s.ain, n_a)
+    for h in range(2):
+        mm(bank(1 + h, H), a_of[row][0], a_of[row][1], 0, T.bq, T.bs, H * h, H * h + H, True, False)
+    if row == col:
+        t.wait_ge(s.ain, n_a)
+    t.wait_ge(s.bin, sum(len(engines(topo.mask(q, core))) for q in relays_of(col_mate, core, cores, topo)))
+    for h in range(2):
+        mm(bank(1 + h, H), a_of[1 - row][0], a_of[1 - row][1], 0, T.ibq, T.ibs, H * h, H * h + H,
+           False, True).then_inc(s["y%d" % h], 1)
+
+    e_rel = engines(topo.mask(core, rel[0]))
+    half = len(e_rel) // 2
+    g.wait_ge(s.qb, 1)
+    send_first(g, T, topo, core, rel[0], T.bq, T.rq, s.rin, e_rel[:half])
+    send_rest(g, T, topo, core, rel[1], T.bq, T.bs, T.rq, T.rs, s.rin, e_rel[half:])
+    e_mate = engines(topo.mask(core, row_mate))
+    rid, pid, _ = topo.addr(row_mate)
+    g.wait_ge(s.qa, 1)
+    g.remote_dma(codes(T.iaq, 0, NA), codes(T.aq, 0, NA), s.ain, s.left, pid, rid, sum(e_mate))
+    g.remote_dma(T.ias[:, 0:NA], T.as_[:, 0:NA], s.ain, s.left, pid, rid, sum(e_mate))
+    g.wait_ge(s.left, len(e_rel) + 2 * len(e_mate))
+
+    g.sync.wait_ge(s.c0, 1)
+    g.sync.dma_start(T.y[:, 0:H], T.yo[:, 0:H]).then_inc(s.st0, 16)
+    g.sync.wait_ge(s.st0, 16)

@@ -1,12 +1,10 @@
 import numpy as np
-from concourse.bass import DstId, RemoteDMATransfer
 from concourse.mybir import dt, AluOpType, ActivationFunctionType
 
 GR = 2
 NA, NB, G = 128, 256, 4
 W = 4 * NA
 H = NB // 2
-CUT = NB - NB // 4
 C = float(np.float32(0.041))
 CORES_SIM = 96
 
@@ -29,10 +27,12 @@ SCRATCH = {
     "yo": ("sbuf", [128, NB], "float32"),
     "ps": ("psum", [128, 512 * 8], "float32"),
 }
-SEMAPHORES = (["lxb", "lwb01", "lwb2", "lwb3", "lxa", "lwa01", "lwa2", "lwa3"]
-              + ["qxb", "qxa", "qa", "qb"] + ["qwb%d" % i for i in range(G)] + ["qwa%d" % i for i in range(G)]
-              + ["mb0", "mb1", "mb2", "mb30", "mb31"] + ["ma%d" % i for i in range(G)] + ["rb", "ra"]
-              + ["y0", "y1", "c0", "c1", "st0", "st1", "left", "ain", "bin", "rin"])
+SEMAPHORES = (["lxb0", "lxb1", "lwb01", "lwb2", "lwb3", "lxa", "lwa01", "lwa2", "lwa3"]
+              + ["qxb0", "qxb1", "qxa", "qa", "qb0", "qb1"] + ["qwb%d" % i for i in range(G)]
+              + ["qwa%d" % i for i in range(G)]
+              + ["mb%d%d" % (h, i) for h in range(2) for i in range(G)] + ["ma%d" % i for i in range(G)]
+              + ["rb0", "rb1", "ra", "y0", "y1", "c0", "c1", "st0", "st1", "left", "ain"]
+              + ["bin0", "bin1", "rin0", "rin1"])
 
 
 def engines(mask):
@@ -40,32 +40,26 @@ def engines(mask):
 
 
 def relays_of(src, dst, cores, topo):
-    return [q for q in range(CORES_SIM) if q not in cores and topo.chip(q) == topo.chip(src)
-            and topo.die(q) == topo.die(src) and topo.may_write(q, dst)][:2]
+    may = [q for q in range(CORES_SIM) if q not in cores and topo.die(q) == topo.die(src) and topo.may_write(q, dst)]
+    near = [q for q in may if topo.chip(q) == topo.chip(src)]
+    far = [q for q in may if topo.same_plane(topo.chip(q), topo.chip(src)) and topo.mates(topo.chip(q), topo.chip(dst))]
+    return [far[0], near[0]]
 
 
-def did(core, topo):
-    rid, pid, _ = topo.addr(core)
-    return DstId(rid=rid, pnc=pid)
+def engines_to(src, rel, topo):
+    far = engines(topo.mask(src, rel[0]))
+    return [far, [e for e in engines(topo.mask(src, rel[1])) if e not in far]]
 
 
-def codes(buf, a, b):
-    return buf[:, a:b].bitcast(dt.uint8)
-
-
-def send_first(g, T, topo, src, dst, src_q, dst_q, sem, eng):
+def put_codes(g, topo, dst, out, in_, h, sem, left, eng):
     rid, pid, _ = topo.addr(dst)
-    g.remote_dma(codes(dst_q, 0, CUT), codes(src_q, 0, CUT), sem, T.sem.left, pid, rid, sum(eng))
+    g.remote_dma(out[:, H * h:H * h + H].bitcast(dt.uint8), in_[:, H * h:H * h + H].bitcast(dt.uint8), sem, left,
+                 pid, rid, sum(eng))
 
 
-def send_rest(g, T, topo, src, dst, src_q, src_s, dst_q, dst_s, sem, eng):
-    h = len(eng) // 2
-    g.remote_dma_fused([
-        RemoteDMATransfer(dst_ids=[did(dst, topo)], dma_engine_mask=sum(eng[:h]), remote_sem=sem,
-                          src=codes(src_q, CUT, NB), dst=codes(dst_q, CUT, NB)),
-        RemoteDMATransfer(dst_ids=[did(dst, topo)], dma_engine_mask=sum(eng[h:]), remote_sem=sem,
-                          src=src_s[:, 0:NB], dst=dst_s[:, 0:NB]),
-    ], local_sem=T.sem.left)
+def put_scales(g, topo, dst, out, in_, h, sem, left, eng):
+    rid, pid, _ = topo.addr(dst)
+    g.remote_dma(out[:, H * h:H * h + H], in_[:, H * h:H * h + H], sem, left, pid, rid, sum(eng))
 
 
 def rank_program(g, core, T, topo):
@@ -77,14 +71,16 @@ def rank_program(g, core, T, topo):
             dst = cores[(r + GR) % (GR * GR)]
             rel = relays_of(src, dst, cores, topo)
             if core in rel:
+                k = rel.index(core)
+                n_in = len(engines_to(src, rel, topo)[k])
                 eng = engines(topo.mask(core, dst))
-                n_in = len(engines(topo.mask(src, core))) // 2
-                g.wait_ge(s.rin, n_in)
-                if core == rel[0]:
-                    send_first(g, T, topo, core, dst, T.rq, T.ibq, s.bin, eng)
-                else:
-                    send_rest(g, T, topo, core, dst, T.rq, T.rs, T.ibq, T.ibs, s.bin, eng)
-                g.wait_ge(s.left, len(eng))
+                for h in range(2):
+                    g.wait_ge(s["rin%d" % h], n_in)
+                    if h == k:
+                        put_codes(g, topo, dst, T.ibq, T.rq, h, s["bin%d" % h], s.left, eng)
+                    else:
+                        put_scales(g, topo, dst, T.ibs, T.rs, h, s["bin%d" % h], s.left, eng)
+                g.wait_ge(s.left, 2 * len(eng))
         return
 
     row, col = divmod(rank, GR)
@@ -93,16 +89,16 @@ def rank_program(g, core, T, topo):
     rel = relays_of(core, col_mate, cores, topo)
     PS = T.ps
 
-    def bank(k, n):
-        return PS[:, 512 * k:512 * k + n]
+    def bank(k):
+        return PS[:, 512 * k:512 * k + H]
 
-    g.sync.dma_start(T.txb[:], T.xb[:]).then_inc(s.lxb, 16)
-    g.scalar.dma_start(T.twb[:, 0:2 * W], T.wb[:, 0:2 * W]).then_inc(s.lwb01, 16)
+    g.scalar.dma_start(T.txb[:, 0:4 * H], T.xb[:, 0:4 * H]).then_inc(s.lxb0, 16)
+    g.sync.dma_start(T.twb[:, 0:2 * W], T.wb[:, 0:2 * W]).then_inc(s.lwb01, 16)
     g.sync.dma_start(T.twb[:, 2 * W:3 * W], T.wb[:, 2 * W:3 * W]).then_inc(s.lwb2, 16)
-    g.scalar.dma_start(T.twb[:, 3 * W:4 * W], T.wb[:, 3 * W:4 * W]).then_inc(s.lwb3, 16)
+    g.sync.dma_start(T.twb[:, 3 * W:4 * W], T.wb[:, 3 * W:4 * W]).then_inc(s.lwb3, 16)
+    g.sync.dma_start(T.txb[:, 4 * H:4 * NB], T.xb[:, 4 * H:4 * NB]).then_inc(s.lxb1, 16)
     g.sync.dma_start(T.txa[:], T.xa[:]).then_inc(s.lxa, 16)
     g.sync.dma_start(T.twa[:, 0:2 * W], T.wa[:, 0:2 * W]).then_inc(s.lwa01, 16)
-    g.sync.wait_ge(s.qb, 1)
     g.sync.dma_start(T.twa[:, 2 * W:3 * W], T.wa[:, 2 * W:3 * W]).then_inc(s.lwa2, 16)
     g.sync.dma_start(T.twa[:, 3 * W:4 * W], T.wa[:, 3 * W:4 * W]).then_inc(s.lwa3, 16)
 
@@ -111,103 +107,104 @@ def rank_program(g, core, T, topo):
     def vrelu(out, in_):
         return v.tensor_scalar(out, in_, 0.0, C, AluOpType.max, AluOpType.mult)
 
-    def quant_w(which, i):
-        t, q, p = {"a": (T.twa, T.waq, T.was), "b": (T.twb, T.wbq, T.wbs)}[which]
-        v.quantize_mx(q[:, 128 * i:128 * i + 128], p[:, 128 * i:128 * i + 128],
-                      t[:, W * i:W * i + W]).then_inc(s["qw%s%d" % (which, i)], 1)
+    def quant(q, p, t, i):
+        return v.quantize_mx(q[:, 128 * i:128 * i + 128], p[:, 128 * i:128 * i + 128], t[:, W * i:W * i + W])
 
-    v.wait_ge(s.lxb, 16)
-    v.quantize_mx(T.xbq[:, 0:NB], T.xbs[:, 0:NB], T.txb[:, 0:4 * NB]).then_inc(s.qxb, 1)
+    def r_of(h, i):
+        return T.tb[:, 4 * H * h + i:4 * H * (h + 1):4]
+
+    v.wait_ge(s.lxb0, 16)
+    quant(T.xbq, T.xbs, T.txb, 0).then_inc(s.qxb0, 1)
     v.wait_ge(s.lwb01, 16)
-    quant_w("b", 0)
-    quant_w("b", 1)
+    quant(T.wbq, T.wbs, T.twb, 0).then_inc(s.qwb0, 1)
+    quant(T.wbq, T.wbs, T.twb, 1).then_inc(s.qwb1, 1)
     v.wait_ge(s.lwb2, 16)
-    quant_w("b", 2)
-    v.wait_ge(s.mb1, 1)
-    vrelu(T.tb[:, 1:4 * NB:4], bank(1, NB)).then_inc(s.rb, 1)
+    quant(T.wbq, T.wbs, T.twb, 2).then_inc(s.qwb2, 1)
     v.wait_ge(s.lwb3, 16)
-    quant_w("b", 3)
-    v.wait_ge(s.mb31, 1)
-    vrelu(T.tb[:, 4 * H + 3:4 * NB:4], bank(4, H)).then_inc(s.rb, 1)
-    v.wait_ge(s.rb, 5)
-    v.quantize_mx(T.bq[:, 0:NB], T.bs[:, 0:NB], T.tb[:, 0:4 * NB]).then_inc(s.qb, 1)
+    quant(T.wbq, T.wbs, T.twb, 3).then_inc(s.qwb3, 1)
+    v.wait_ge(s.lxb1, 16)
+    quant(T.xbq, T.xbs, T.txb, 1).then_inc(s.qxb1, 1)
+    v.wait_ge(s.rb0, 4)
+    quant(T.bq, T.bs, T.tb, 0).then_inc(s.qb0, 1)
+    for i in (1, 3):
+        v.wait_ge(s["mb1%d" % i], 1)
+        vrelu(r_of(1, i), bank(4 + i)).then_inc(s.rb1, 1)
+    v.wait_ge(s.rb1, 4)
+    quant(T.bq, T.bs, T.tb, 1).then_inc(s.qb1, 1)
     v.wait_ge(s.lxa, 16)
-    v.quantize_mx(T.xaq[:, 0:NA], T.xas[:, 0:NA], T.txa[:, 0:4 * NA]).then_inc(s.qxa, 1)
+    quant(T.xaq, T.xas, T.txa, 0).then_inc(s.qxa, 1)
     v.wait_ge(s.lwa01, 16)
-    quant_w("a", 0)
-    quant_w("a", 1)
+    quant(T.waq, T.was, T.twa, 0).then_inc(s.qwa0, 1)
+    quant(T.waq, T.was, T.twa, 1).then_inc(s.qwa1, 1)
     v.wait_ge(s.lwa2, 16)
-    quant_w("a", 2)
+    quant(T.waq, T.was, T.twa, 2).then_inc(s.qwa2, 1)
     v.wait_ge(s.lwa3, 16)
-    quant_w("a", 3)
+    quant(T.waq, T.was, T.twa, 3).then_inc(s.qwa3, 1)
     v.wait_ge(s.ma3, 1)
-    vrelu(T.ta[:, 3:4 * NA:4], bank(0, NA)).then_inc(s.ra, 1)
+    vrelu(T.ta[:, 3:4 * NA:4], bank(3)).then_inc(s.ra, 1)
     v.wait_ge(s.ra, 4)
-    v.quantize_mx(T.aq[:, 0:NA], T.as_[:, 0:NA], T.ta[:, 0:4 * NA]).then_inc(s.qa, 1)
+    quant(T.aq, T.as_, T.ta, 0).then_inc(s.qa, 1)
     v.wait_ge(s.y0, 1)
-    v.tensor_copy(T.yo[:, 0:H], bank(1, H)).then_inc(s.c0, 1)
+    v.tensor_copy(T.yo[:, 0:H], bank(4)).then_inc(s.c0, 1)
 
     sc = g.scalar
     relu, copy = ActivationFunctionType.Relu, ActivationFunctionType.Copy
-    sc.wait_ge(s.mb0, 1)
-    sc.activation(T.tb[:, 0:4 * NB:4], bank(0, NB), relu, scale=C).then_inc(s.rb, 1)
-    sc.wait_ge(s.mb2, 1)
-    sc.activation(T.tb[:, 2:4 * NB:4], bank(2, NB), relu, scale=C).then_inc(s.rb, 1)
-    sc.wait_ge(s.mb30, 1)
-    sc.activation(T.tb[:, 3:4 * H:4], bank(3, H), relu, scale=C).then_inc(s.rb, 1)
+    for h, i in ((0, 0), (0, 1), (0, 2), (0, 3), (1, 0), (1, 2)):
+        sc.wait_ge(s["mb%d%d" % (h, i)], 1)
+        sc.activation(r_of(h, i), bank(4 * h + i), relu, scale=C).then_inc(s["rb%d" % h], 1)
     for i in range(G - 1):
         sc.wait_ge(s["ma%d" % i], 1)
-        sc.activation(T.ta[:, i:4 * NA:4], bank(5 + i, NA), relu, scale=C).then_inc(s.ra, 1)
+        sc.activation(T.ta[:, i:4 * NA:4], bank(i), relu, scale=C).then_inc(s.ra, 1)
     sc.wait_ge(s.y1, 1)
-    sc.activation(T.yo[:, H:NB], bank(2, H), copy).then_inc(s.c1, 1)
+    sc.activation(T.yo[:, H:NB], bank(5), copy).then_inc(s.c1, 1)
     sc.wait_ge(s.c1, 1)
     sc.dma_start(T.y[:, H:NB], T.yo[:, H:NB]).then_inc(s.st1, 16)
     sc.wait_ge(s.st1, 16)
 
     t = g.tensor
 
-    def mm(out, q, p, i, xq, xp, a, b, start=True, stop=True):
+    def mm(out, q, p, i, xq, xp, h, start=True, stop=True):
         return t.matmul_mx(out, q[:, 128 * i:128 * i + 128], p[:, 128 * i:128 * i + 128],
-                           xq[:, a:b], xp[:, a:b], start, stop)
+                           xq[:, H * h:H * h + H], xp[:, H * h:H * h + H], start, stop)
 
-    t.wait_ge(s.qxb, 1)
-    for i in range(G - 1):
-        t.wait_ge(s["qwb%d" % i], 1)
-        mm(bank(i, NB), T.wbq, T.wbs, i, T.xbq, T.xbs, 0, NB).then_inc(s["mb%d" % i], 1)
-    t.wait_ge(s.qwb3, 1)
-    mm(bank(3, H), T.wbq, T.wbs, 3, T.xbq, T.xbs, 0, H).then_inc(s.mb30, 1)
-    mm(bank(4, H), T.wbq, T.wbs, 3, T.xbq, T.xbs, H, NB).then_inc(s.mb31, 1)
+    for h in range(2):
+        t.wait_ge(s["qxb%d" % h], 1)
+        for i in range(G):
+            if h == 0:
+                t.wait_ge(s["qwb%d" % i], 1)
+            mm(bank(4 * h + i), T.wbq, T.wbs, i, T.xbq, T.xbs, h).then_inc(s["mb%d%d" % (h, i)], 1)
     t.wait_ge(s.qxa, 1)
-    t.wait_ge(s.rb, 5)
+    t.wait_ge(s.rb0, 4)
     for i in range(G):
         t.wait_ge(s["qwa%d" % i], 1)
-        mm(bank((5, 6, 7, 0)[i], NA), T.waq, T.was, i, T.xaq, T.xas, 0, NA).then_inc(s["ma%d" % i], 1)
+        mm(bank(i), T.waq, T.was, i, T.xaq, T.xas, 0).then_inc(s["ma%d" % i], 1)
     a_of = {col: (T.aq, T.as_), 1 - col: (T.iaq, T.ias)}
-    t.wait_ge(s.qb, 1)
+    t.wait_ge(s.rb1, 4)
+    t.wait_ge(s.qb0, 1)
+    t.wait_ge(s.qb1, 1)
     t.wait_ge(s.qa, 1)
     n_a = 2 * len(engines(topo.mask(row_mate, core)))
     if row != col:
         t.wait_ge(s.ain, n_a)
     for h in range(2):
-        mm(bank(1 + h, H), a_of[row][0], a_of[row][1], 0, T.bq, T.bs, H * h, H * h + H, True, False)
+        mm(bank(4 + h), a_of[row][0], a_of[row][1], 0, T.bq, T.bs, h, True, False)
     if row == col:
         t.wait_ge(s.ain, n_a)
-    t.wait_ge(s.bin, sum(len(engines(topo.mask(q, core))) for q in relays_of(col_mate, core, cores, topo)))
+    n_b = sum(len(engines(topo.mask(q, core))) for q in relays_of(col_mate, core, cores, topo))
     for h in range(2):
-        mm(bank(1 + h, H), a_of[1 - row][0], a_of[1 - row][1], 0, T.ibq, T.ibs, H * h, H * h + H,
-           False, True).then_inc(s["y%d" % h], 1)
+        t.wait_ge(s["bin%d" % h], n_b)
+        mm(bank(4 + h), a_of[1 - row][0], a_of[1 - row][1], 0, T.ibq, T.ibs, h, False, True).then_inc(s["y%d" % h], 1)
 
-    e_rel = engines(topo.mask(core, rel[0]))
-    half = len(e_rel) // 2
-    g.wait_ge(s.qb, 1)
-    send_first(g, T, topo, core, rel[0], T.bq, T.rq, s.rin, e_rel[:half])
-    send_rest(g, T, topo, core, rel[1], T.bq, T.bs, T.rq, T.rs, s.rin, e_rel[half:])
+    e_rel = engines_to(core, rel, topo)
+    for h in range(2):
+        g.wait_ge(s["qb%d" % h], 1)
+        put_codes(g, topo, rel[h], T.rq, T.bq, h, s["rin%d" % h], s.left, e_rel[h])
+        put_scales(g, topo, rel[1 - h], T.rs, T.bs, h, s["rin%d" % h], s.left, e_rel[1 - h])
     e_mate = engines(topo.mask(core, row_mate))
-    rid, pid, _ = topo.addr(row_mate)
     g.wait_ge(s.qa, 1)
-    g.remote_dma(codes(T.iaq, 0, NA), codes(T.aq, 0, NA), s.ain, s.left, pid, rid, sum(e_mate))
-    g.remote_dma(T.ias[:, 0:NA], T.as_[:, 0:NA], s.ain, s.left, pid, rid, sum(e_mate))
-    g.wait_ge(s.left, len(e_rel) + 2 * len(e_mate))
+    put_codes(g, topo, row_mate, T.iaq, T.aq, 0, s.ain, s.left, e_mate)
+    put_scales(g, topo, row_mate, T.ias, T.as_, 0, s.ain, s.left, e_mate)
+    g.wait_ge(s.left, 2 * len(e_rel[0]) + 2 * len(e_rel[1]) + 2 * len(e_mate))
 
     g.sync.wait_ge(s.c0, 1)
     g.sync.dma_start(T.y[:, 0:H], T.yo[:, 0:H]).then_inc(s.st0, 16)

import numpy as np
from concourse.mybir import dt, AluOpType, ActivationFunctionType

GR = 2
NA, NB, G = 128, 256, 4
W = 4 * NA
H = NB // 2
C = float(np.float32(0.041))
CORES_SIM = 96

SCRATCH = {
    "txa": ("sbuf", [128, 4 * NA], "bfloat16"),
    "txb": ("sbuf", [128, 4 * NB], "bfloat16"),
    "twa": ("sbuf", [128, G * W], "bfloat16"),
    "twb": ("sbuf", [128, G * W], "bfloat16"),
    "ta": ("sbuf", [128, 4 * NA], "bfloat16"),
    "tb": ("sbuf", [128, 4 * NB], "bfloat16"),
    "xaq": ("sbuf", [128, NA], "float8_e4m3fn_x4"), "xas": ("sbuf", [128, NA], "uint8"),
    "xbq": ("sbuf", [128, NB], "float8_e4m3fn_x4"), "xbs": ("sbuf", [128, NB], "uint8"),
    "waq": ("sbuf", [128, G * 128], "float8_e4m3fn_x4"), "was": ("sbuf", [128, G * 128], "uint8"),
    "wbq": ("sbuf", [128, G * 128], "float8_e4m3fn_x4"), "wbs": ("sbuf", [128, G * 128], "uint8"),
    "aq": ("sbuf", [128, NA], "float8_e4m3fn_x4"), "as_": ("sbuf", [128, NA], "uint8"),
    "bq": ("sbuf", [128, NB], "float8_e4m3fn_x4"), "bs": ("sbuf", [128, NB], "uint8"),
    "iaq": ("sbuf", [128, NA], "float8_e4m3fn_x4"), "ias": ("sbuf", [128, NA], "uint8"),
    "ibq": ("sbuf", [128, NB], "float8_e4m3fn_x4"), "ibs": ("sbuf", [128, NB], "uint8"),
    "rq": ("sbuf", [128, NB], "float8_e4m3fn_x4"), "rs": ("sbuf", [128, NB], "uint8"),
    "yo": ("sbuf", [128, NB], "float32"),
    "ps": ("psum", [128, 512 * 8], "float32"),
}
SEMAPHORES = (["lxb0", "lxb1", "lwb01", "lwb2", "lwb3", "lxa", "lwa01", "lwa2", "lwa3"]
              + ["qxb0", "qxb1", "qxa", "qa", "qb0", "qb1"] + ["qwb%d" % i for i in range(G)]
              + ["qwa%d" % i for i in range(G)]
              + ["mb%d%d" % (h, i) for h in range(2) for i in range(G)] + ["ma%d" % i for i in range(G)]
              + ["rb0", "rb1", "ra", "y0", "y1", "c0", "c1", "st0", "st1", "left", "ain"]
              + ["bin0", "bin1", "rin0", "rin1"])


def engines(mask):
    return [1 << e for e in range(mask.bit_length()) if mask >> e & 1]


def relays_of(src, dst, cores, topo):
    may = [q for q in range(CORES_SIM) if q not in cores and topo.die(q) == topo.die(src) and topo.may_write(q, dst)]
    near = [q for q in may if topo.chip(q) == topo.chip(src)]
    far = [q for q in may if topo.same_plane(topo.chip(q), topo.chip(src)) and topo.mates(topo.chip(q), topo.chip(dst))]
    return [far[0], near[0]]


def engines_to(src, rel, topo):
    far = engines(topo.mask(src, rel[0]))
    return [far, [e for e in engines(topo.mask(src, rel[1])) if e not in far]]


def put_codes(g, topo, dst, out, in_, h, sem, left, eng):
    rid, pid, _ = topo.addr(dst)
    g.remote_dma(out[:, H * h:H * h + H].bitcast(dt.uint8), in_[:, H * h:H * h + H].bitcast(dt.uint8), sem, left,
                 pid, rid, sum(eng))


def put_scales(g, topo, dst, out, in_, h, sem, left, eng):
    rid, pid, _ = topo.addr(dst)
    g.remote_dma(out[:, H * h:H * h + H], in_[:, H * h:H * h + H], sem, left, pid, rid, sum(eng))


def rank_program(g, core, T, topo):
    cores = list(T.cores)
    rank = T.rank_of(core)
    s = T.sem
    if rank is None:
        for r, src in enumerate(cores):
            dst = cores[(r + GR) % (GR * GR)]
            rel = relays_of(src, dst, cores, topo)
            if core in rel:
                k = rel.index(core)
                n_in = len(engines_to(src, rel, topo)[k])
                eng = engines(topo.mask(core, dst))
                for h in range(2):
                    g.wait_ge(s["rin%d" % h], n_in)
                    if h == k:
                        put_codes(g, topo, dst, T.ibq, T.rq, h, s["bin%d" % h], s.left, eng)
                    else:
                        put_scales(g, topo, dst, T.ibs, T.rs, h, s["bin%d" % h], s.left, eng)
                g.wait_ge(s.left, 2 * len(eng))
        return

    row, col = divmod(rank, GR)
    row_mate = cores[GR * row + 1 - col]
    col_mate = cores[GR * (1 - row) + col]
    rel = relays_of(core, col_mate, cores, topo)
    PS = T.ps

    def bank(k):
        return PS[:, 512 * k:512 * k + H]

    g.scalar.dma_start(T.txb[:, 0:4 * H], T.xb[:, 0:4 * H]).then_inc(s.lxb0, 16)
    g.sync.dma_start(T.twb[:, 0:2 * W], T.wb[:, 0:2 * W]).then_inc(s.lwb01, 16)
    g.sync.dma_start(T.twb[:, 2 * W:3 * W], T.wb[:, 2 * W:3 * W]).then_inc(s.lwb2, 16)
    g.sync.dma_start(T.twb[:, 3 * W:4 * W], T.wb[:, 3 * W:4 * W]).then_inc(s.lwb3, 16)
    g.sync.dma_start(T.txb[:, 4 * H:4 * NB], T.xb[:, 4 * H:4 * NB]).then_inc(s.lxb1, 16)
    g.sync.dma_start(T.txa[:], T.xa[:]).then_inc(s.lxa, 16)
    g.sync.dma_start(T.twa[:, 0:2 * W], T.wa[:, 0:2 * W]).then_inc(s.lwa01, 16)
    g.sync.dma_start(T.twa[:, 2 * W:3 * W], T.wa[:, 2 * W:3 * W]).then_inc(s.lwa2, 16)
    g.sync.dma_start(T.twa[:, 3 * W:4 * W], T.wa[:, 3 * W:4 * W]).then_inc(s.lwa3, 16)

    v = g.vector

    def vrelu(out, in_):
        return v.tensor_scalar(out, in_, 0.0, C, AluOpType.max, AluOpType.mult)

    def quant(q, p, t, i):
        return v.quantize_mx(q[:, 128 * i:128 * i + 128], p[:, 128 * i:128 * i + 128], t[:, W * i:W * i + W])

    def r_of(h, i):
        return T.tb[:, 4 * H * h + i:4 * H * (h + 1):4]

    v.wait_ge(s.lxb0, 16)
    quant(T.xbq, T.xbs, T.txb, 0).then_inc(s.qxb0, 1)
    v.wait_ge(s.lwb01, 16)
    quant(T.wbq, T.wbs, T.twb, 0).then_inc(s.qwb0, 1)
    quant(T.wbq, T.wbs, T.twb, 1).then_inc(s.qwb1, 1)
    v.wait_ge(s.lwb2, 16)
    quant(T.wbq, T.wbs, T.twb, 2).then_inc(s.qwb2, 1)
    v.wait_ge(s.lwb3, 16)
    quant(T.wbq, T.wbs, T.twb, 3).then_inc(s.qwb3, 1)
    v.wait_ge(s.lxb1, 16)
    quant(T.xbq, T.xbs, T.txb, 1).then_inc(s.qxb1, 1)
    v.wait_ge(s.rb0, 4)
    quant(T.bq, T.bs, T.tb, 0).then_inc(s.qb0, 1)
    for i in (1, 3):
        v.wait_ge(s["mb1%d" % i], 1)
        vrelu(r_of(1, i), bank(4 + i)).then_inc(s.rb1, 1)
    v.wait_ge(s.rb1, 4)
    quant(T.bq, T.bs, T.tb, 1).then_inc(s.qb1, 1)
    v.wait_ge(s.lxa, 16)
    quant(T.xaq, T.xas, T.txa, 0).then_inc(s.qxa, 1)
    v.wait_ge(s.lwa01, 16)
    quant(T.waq, T.was, T.twa, 0).then_inc(s.qwa0, 1)
    quant(T.waq, T.was, T.twa, 1).then_inc(s.qwa1, 1)
    v.wait_ge(s.lwa2, 16)
    quant(T.waq, T.was, T.twa, 2).then_inc(s.qwa2, 1)
    v.wait_ge(s.lwa3, 16)
    quant(T.waq, T.was, T.twa, 3).then_inc(s.qwa3, 1)
    v.wait_ge(s.ma3, 1)
    vrelu(T.ta[:, 3:4 * NA:4], bank(3)).then_inc(s.ra, 1)
    v.wait_ge(s.ra, 4)
    quant(T.aq, T.as_, T.ta, 0).then_inc(s.qa, 1)
    v.wait_ge(s.y0, 1)
    v.tensor_copy(T.yo[:, 0:H], bank(4)).then_inc(s.c0, 1)

    sc = g.scalar
    relu, copy = ActivationFunctionType.Relu, ActivationFunctionType.Copy
    for h, i in ((0, 0), (0, 1), (0, 2), (0, 3), (1, 0), (1, 2)):
        sc.wait_ge(s["mb%d%d" % (h, i)], 1)
        sc.activation(r_of(h, i), bank(4 * h + i), relu, scale=C).then_inc(s["rb%d" % h], 1)
    for i in range(G - 1):
        sc.wait_ge(s["ma%d" % i], 1)
        sc.activation(T.ta[:, i:4 * NA:4], bank(i), relu, scale=C).then_inc(s.ra, 1)
    sc.wait_ge(s.y1, 1)
    sc.activation(T.yo[:, H:NB], bank(5), copy).then_inc(s.c1, 1)
    sc.wait_ge(s.c1, 1)
    sc.dma_start(T.y[:, H:NB], T.yo[:, H:NB]).then_inc(s.st1, 16)
    sc.wait_ge(s.st1, 16)

    t = g.tensor

    def mm(out, q, p, i, xq, xp, h, start=True, stop=True):
        return t.matmul_mx(out, q[:, 128 * i:128 * i + 128], p[:, 128 * i:128 * i + 128],
                           xq[:, H * h:H * h + H], xp[:, H * h:H * h + H], start, stop)

    for h in range(2):
        t.wait_ge(s["qxb%d" % h], 1)
        for i in range(G):
            if h == 0:
                t.wait_ge(s["qwb%d" % i], 1)
            mm(bank(4 * h + i), T.wbq, T.wbs, i, T.xbq, T.xbs, h).then_inc(s["mb%d%d" % (h, i)], 1)
    t.wait_ge(s.qxa, 1)
    t.wait_ge(s.rb0, 4)
    for i in range(G):
        t.wait_ge(s["qwa%d" % i], 1)
        mm(bank(i), T.waq, T.was, i, T.xaq, T.xas, 0).then_inc(s["ma%d" % i], 1)
    a_of = {col: (T.aq, T.as_), 1 - col: (T.iaq, T.ias)}
    t.wait_ge(s.rb1, 4)
    t.wait_ge(s.qb0, 1)
    t.wait_ge(s.qb1, 1)
    t.wait_ge(s.qa, 1)
    n_a = 2 * len(engines(topo.mask(row_mate, core)))
    if row != col:
        t.wait_ge(s.ain, n_a)
    for h in range(2):
        mm(bank(4 + h), a_of[row][0], a_of[row][1], 0, T.bq, T.bs, h, True, False)
    if row == col:
        t.wait_ge(s.ain, n_a)
    n_b = sum(len(engines(topo.mask(q, core))) for q in relays_of(col_mate, core, cores, topo))
    for h in range(2):
        t.wait_ge(s["bin%d" % h], n_b)
        mm(bank(4 + h), a_of[1 - row][0], a_of[1 - row][1], 0, T.ibq, T.ibs, h, False, True).then_inc(s["y%d" % h], 1)

    e_rel = engines_to(core, rel, topo)
    for h in range(2):
        g.wait_ge(s["qb%d" % h], 1)
        put_codes(g, topo, rel[h], T.rq, T.bq, h, s["rin%d" % h], s.left, e_rel[h])
        put_scales(g, topo, rel[1 - h], T.rs, T.bs, h, s["rin%d" % h], s.left, e_rel[1 - h])
    e_mate = engines(topo.mask(core, row_mate))
    g.wait_ge(s.qa, 1)
    put_codes(g, topo, row_mate, T.iaq, T.aq, 0, s.ain, s.left, e_mate)
    put_scales(g, topo, row_mate, T.ias, T.as_, 0, s.ain, s.left, e_mate)
    g.wait_ge(s.left, 2 * len(e_rel[0]) + 2 * len(e_rel[1]) + 2 * len(e_mate))

    g.sync.wait_ge(s.c0, 1)
    g.sync.dma_start(T.y[:, 0:H], T.yo[:, 0:H]).then_inc(s.st0, 16)
    g.sync.wait_ge(s.st0, 16)
